import numpy as np
import ml_dtypes


def mxq(x, axis, fmt="e4m3"):
    dtype, down = {"e4m3": (ml_dtypes.float8_e4m3fn, 7), "e5m2": (ml_dtypes.float8_e5m2, 14)}[fmt]
    v = np.moveaxis(np.asarray(x, np.float32).astype(ml_dtypes.bfloat16).astype(np.float64), axis, -1)
    blocks = v.reshape(v.shape[:-1] + (-1, 32))
    amax = np.abs(blocks).max(-1, keepdims=True)
    byte = np.maximum(np.where(amax > 0, np.frexp(amax)[1] - 1 + 127, 0) - down, 1)
    scale = np.exp2(byte - 127.0)
    codes = (blocks / scale).astype(np.float32).astype(dtype).astype(np.float64)
    return np.moveaxis((codes * scale).reshape(v.shape), -1, axis)


WIDE = False


def mx_kscale(k):
    if not WIDE:
        return np.ones(k)
    levels = np.array([10, -10, 5, -5, 0])
    if k % 512:
        return np.exp2(np.random.permutation(np.resize(levels, k // 32))).repeat(32)
    a = np.empty((k // 512, 16))
    for p in range(k // 512):
        a[p, :8] = np.random.permutation(np.resize(levels, 8))
        for g in range(8):
            far = levels[np.abs(levels - a[p, g]) >= 10]
            a[p, g + 8] = far[np.random.randint(len(far))]
    return np.exp2(a.ravel()).repeat(32)


def f64(x):
    return np.asarray(x).astype(np.float64)


def striped(idx):
    return np.tile(idx.reshape(-1, 16).T, (8, 1)).astype(np.uint16)


def unstriped(offs):
    return offs[:16].T.reshape(-1).astype(np.int64)


E2M1 = np.array([0.0, 0.5, 1.0, 1.5, 2.0, 3.0, 4.0, 6.0, -0.0, -0.5, -1.0, -1.5, -2.0, -3.0, -4.0, -6.0])


def pack_weight(w, fmt):
    k, n = w.shape
    w = f64(np.asarray(w, np.float32).astype(ml_dtypes.bfloat16)).reshape(k // 32, 32, n)
    amax = np.abs(w).max(1)
    if fmt == "e4m3":
        byte = np.frexp(amax)[1] - 1 + 127 - 7
    else:
        mant, ex = np.frexp(amax / 6.0)
        byte = np.where(mant > 0.5, ex, ex - 1) + 127
    byte = np.clip(np.where(amax > 0, byte, 1), 1, 254)
    scaled = (w * np.exp2(127.0 - byte)[:, None, :]).reshape(k, n).astype(np.float32)
    by_word = np.ascontiguousarray(scaled.reshape(k // 512, 128, 4, n).transpose(0, 1, 3, 2))
    if fmt == "e4m3":
        words = by_word.astype(ml_dtypes.float8_e4m3fn).view(np.uint8)
    else:
        c = by_word.astype(ml_dtypes.float4_e2m1fn).view(np.uint8) & 0xF
        words = (c[..., 0::2] | (c[..., 1::2] << 4)).reshape(k // 512, 128, 2 * n)
    return np.ascontiguousarray(words), np.ascontiguousarray(byte.astype(np.uint8).reshape(k // 512, 16, n))


def unpack_weight(words, scales, fmt):
    g, _, n = scales.shape
    words = np.ascontiguousarray(words).reshape(g, 128, n, -1)
    if fmt == "e4m3":
        vals = words.view(ml_dtypes.float8_e4m3fn).astype(np.float64)
    else:
        nib = np.empty((g, 128, n, 4), np.uint8)
        nib[..., 0::2] = words & 0xF
        nib[..., 1::2] = words >> 4
        vals = E2M1[nib]
    vals = vals * np.repeat(np.exp2(scales.astype(np.float64) - 127.0), 8, axis=1)[..., None]
    return vals.transpose(0, 1, 3, 2).reshape(g * 512, n)


def gelu(v):
    return 0.5 * v * (1.0 + np.tanh(np.sqrt(2.0 / np.pi) * (v + 0.044715 * v**3)))


def striped8(idx):
    return np.concatenate([v.reshape(-1, 16).T for v in idx]).astype(np.uint16)


def unstriped8(offs):
    return np.stack([offs[16 * g:16 * g + 16].T.reshape(-1) for g in range(8)]).astype(np.int64)


def heads(h, wgt, idx8):
    r = np.arange(h.shape[0])
    return wgt[r // 4 % 128] * h[r[:, None], idx8[r % 512 // 64]]


K, T, S, T2, P, H, N = 1024, 2048, 1024, 2048, 1024, 512, 512

def setup_inputs():
    n = np.random.standard_normal
    s = mx_kscale(K)[:, None]
    u = mx_kscale(H)[:, None]
    tab_words, tab_scales = pack_weight(n((K, T)) * s, "e4m3")
    w4_words, w4_scales = pack_weight(n((H, N)) / np.sqrt(H) / u, "e2m1")
    return {
        "tab_words": tab_words, "tab_scales": tab_scales,
        "offs": striped(np.random.permutation(T)[:S]),
        "w1": (0.4 * n((K, H)) / np.sqrt(K) / s).astype(np.float32),
        "b1": np.random.uniform(-0.8, 0.8, H).astype(np.float32),
        "gain": (2.0 * np.exp(0.3 * n(H)) * u[:, 0]).astype(np.float32),
        "page0": (n((H, T2)) * u).astype(np.float32),
        "wgs": np.exp(0.3 * n((128, S))).astype(np.float32),
        "offs2": striped(np.random.permutation(T2)[:S]),
        "wgt": np.repeat(np.random.uniform(0.5, 2.0, (8, P)), 16, axis=0).astype(np.float32),
        "offs3": striped8(np.stack([np.random.permutation(T2)[:P] for _ in range(8)])),
        "w4_words": w4_words, "w4_scales": w4_scales,
        "w5": (n((H, N)) / np.sqrt(H) / u).astype(np.float32),
    }

def reference(tab_words, tab_scales, offs, w1, b1, gain, page0, wgs, offs2, wgt, offs3,
              w4_words, w4_scales, w5):
    v = unpack_weight(tab_words, tab_scales, "e4m3")[:, unstriped(offs)]
    w1q = mxq(f64(w1), 0, "e4m3")
    a = (w1q.T @ v) + f64(b1)[:, None]
    h = f64(gain)[:, None] * (a * np.cos(a))
    page = f64(page0).copy()
    page[:, unstriped(offs2)] = np.tile(f64(wgs), (H // 128, 1)) * h
    x = heads(page, f64(wgt), unstriped8(offs3))
    xq = mxq(x, 0, "e4m3")
    w4 = unpack_weight(w4_words, w4_scales, "e2m1")
    w5q = mxq(f64(w5), 0, "e4m3")
    y1 = w4.T @ xq
    y2 = w5q.T @ xq
    return np.maximum(y1, y2)

@@ -1,0 +1,243 @@
+import math
+from contextlib import ExitStack
+
+import concourse.mybir as mybir
+from concourse.masks import make_identity
+
+K, T, S, T2, M, H, N = 1024, 2048, 1024, 2048, 1024, 512, 512
+FLOPS = 2 * K * H * S + 2 * 2 * H * N * M
+
+F32 = mybir.dt.float32
+BF16 = mybir.dt.bfloat16
+I32 = mybir.dt.int32
+U32 = mybir.dt.uint32
+U16 = mybir.dt.uint16
+U8 = mybir.dt.uint8
+FP8X4 = mybir.dt.float8_e4m3fn_x4
+FP4X4 = mybir.dt.float4_e2m1fn_x4
+ACT = mybir.ActivationFunctionType
+ALU = mybir.AluOpType
+
+P = 128
+PACK = 4
+BANK = 512
+TURN = 2.0 * math.pi
+TURN_SHIFT = 65536.0
+RING = 5
+J_PIECES = [(0, 256), (256, 512), (512, 1024)]
+M_PIECES = [(0, 256), (256, 512), (512, 768), (768, 896), (896, 1024)]
+
+
+def tile_list_drowsiness_warning_features_kernel(
+    tc, tab_words, tab_scales, offs, w1, b1, gain, page0, wgs, offs2, wgt, offs3, w4_words, w4_scales, w5, out
+):
+    nc = tc.nc
+    with ExitStack() as ctx:
+        lists = ctx.enter_context(tc.tile_pool(name="lists", bufs=1))
+        keep = ctx.enter_context(tc.tile_pool(name="keep", bufs=1))
+        work = ctx.enter_context(tc.tile_pool(name="work", bufs=2))
+        psum = ctx.enter_context(tc.psum_pool(name="psum", bufs=1))
+
+        idx = lists.tile([P, S // 16], U16, name="idx")
+        idx2 = lists.tile([P, S // 16], U16, name="idx2")
+        idx3 = lists.tile([P, M // 16], U16, name="idx3")
+
+        tab_plane = keep.tile([P, T], U8, name="tab_plane")
+        nc.vector.memset(tab_plane[:].bitcast(I32), 0)
+        w4_plane = keep.tile([P, N], U8, name="w4_plane", align_bytes=64)
+        nc.gpsimd.memset(w4_plane[:].bitcast(I32), 0)
+        ident = keep.tile([P, P], F32, name="ident")
+        make_identity(nc, ident[:])
+
+        w1_raw = [keep.tile([P, PACK, H], F32, name=f"w1_raw{a}") for a in range(2)]
+        w1_rows = w1.rearrange("(a p i) r -> a p i r", a=2, i=PACK)
+        nc.sync.dma_start(idx[:], offs)
+        nc.sync.dma_start(out=w1_raw[0][:], in_=w1_rows[0])
+        for q in range(4):
+            nc.sync.dma_start(
+                out=tab_plane[32 * q : 32 * q + 8, :].bitcast(I32),
+                in_=tab_scales[:, 4 * q : 4 * q + 4, :].bitcast(I32),
+            )
+        nc.sync.dma_start(out=w1_raw[1][:], in_=w1_rows[1])
+        tab = [keep.tile([P, T], I32, name=f"tab{a}") for a in range(2)]
+        for a in range(2):
+            nc.sync.dma_start(out=tab[a][:], in_=tab_words[a].rearrange("p t i -> p (t i)").bitcast(I32))
+        b1_sb = keep.tile([P, PACK], F32, name="b1_sb")
+        gain_sb = keep.tile([P, PACK], F32, name="gain_sb")
+        nc.sync.dma_start(out=b1_sb[:], in_=b1.rearrange("(p i) -> p i", i=PACK))
+        nc.sync.dma_start(out=gain_sb[:], in_=gain.rearrange("(p i) -> p i", i=PACK))
+        nc.sync.dma_start(idx2[:], offs2)
+        page = [keep.tile([P, T2], F32, name=f"page{i}") for i in range(PACK)]
+        page_rows = page0.rearrange("(p i) c -> p i c", i=PACK)
+        wgs_rows = wgs.rearrange("(s i) j -> s i j", i=PACK)
+        wgs_first = keep.tile([P, S], F32, name="wgs_first")
+        wgs_rest = keep.tile([P, PACK - 1, S], F32, name="wgs_rest")
+        nc.sync.dma_start(out=page[0][:], in_=page_rows[:, 0, :])
+        for q in (0, 2, 1, 3):
+            nc.sync.dma_start(out=wgs_first[32 * q : 32 * q + 32, :], in_=wgs_rows[:, 0, :])
+        nc.sync.dma_start(out=page[1][:], in_=page_rows[:, 1, :])
+        for q in (0, 2, 1, 3):
+            nc.sync.dma_start(out=wgs_rest[32 * q : 32 * q + 32, :, :], in_=wgs_rows[:, 1:, :])
+        nc.sync.dma_start(out=page[2][:], in_=page_rows[:, 2, :])
+        nc.sync.dma_start(out=page[3][:], in_=page_rows[:, 3, :])
+        w5_raw = keep.tile([P, PACK, N], F32, name="w5_raw")
+        nc.sync.dma_start(out=w5_raw[:], in_=w5.rearrange("(p i) n -> p i n", i=PACK))
+        wgt_sb = keep.tile([P, M], F32, name="wgt_sb")
+        nc.sync.dma_start(out=wgt_sb[:], in_=wgt)
+        nc.sync.dma_start(idx3[:], offs3)
+        w4_codes = keep.tile([P, 2 * N], U8, name="w4_codes", align_bytes=64)
+        nc.sync.dma_start(out=w4_codes[:].bitcast(I32), in_=w4_words[0].bitcast(I32))
+        for q in range(4):
+            nc.sync.dma_start(
+                out=w4_plane[32 * q : 32 * q + 4, :].bitcast(I32), in_=w4_scales[0, 4 * q : 4 * q + 4, :].bitcast(I32)
+            )
+
+        w1_bf = [keep.tile([P, PACK * H], BF16, name=f"w1_bf{a}", align_bytes=64) for a in range(2)]
+        w1_codes = [keep.tile([P, H], U32, name=f"w1_codes{a}", align_bytes=64) for a in range(2)]
+        w1_plane = [keep.tile([P, H], U8, name=f"w1_plane{a}", align_bytes=64) for a in range(2)]
+        dealt = [w1_bf[a][:].rearrange("p (t m i) -> p m t i", t=PACK, i=PACK) for a in range(2)]
+        raw = [w1_raw[a][:].rearrange("p i (m t) -> p m t i", t=PACK) for a in range(2)]
+        nc.scalar.copy(out=dealt[0], in_=raw[0])
+        nc.vector.tensor_copy(out=dealt[1][:, 0:64], in_=raw[1][:, 0:64])
+        nc.scalar.copy(out=dealt[1][:, 64:128], in_=raw[1][:, 64:128])
+
+        v_codes = [keep.tile([P, S], U32, name=f"v_codes{a}", align_bytes=64) for a in range(2)]
+        v_plane = keep.tile([P, S], U8, name="v_plane", align_bytes=64)
+        for lo, hi in J_PIECES:
+            nc.vector.tensor_copy(v_plane[:, lo:hi], tab_plane[:].indirect(idx[:, lo // 16 : hi // 16]))
+        for a in range(2):
+            nc.vector.quantize_mx(out=w1_codes[a][:].bitcast(FP8X4), scales=w1_plane[a][:], in_=w1_bf[a][:])
+        for lo, hi in J_PIECES:
+            for a in range(2):
+                nc.vector.tensor_copy(v_codes[a][:, lo:hi], tab[a][:].bitcast(U32).indirect(idx[:, lo // 16 : hi // 16]))
+
+        banks = [psum.tile([P, BANK], F32, name=f"bank{i}") for i in range(8)]
+        vals = [keep.tile([P, BANK], F32, name=f"val{i}") for i in range(RING)]
+
+        def product(t, lo, hi, acc, val):
+            for a in range(2):
+                nc.tensor.matmul_mx(
+                    out=acc,
+                    lhsT=w1_codes[a][:, P * t : P * (t + 1)].bitcast(FP8X4),
+                    lhsT_scale=w1_plane[a][:, P * t : P * (t + 1)],
+                    rhs=v_codes[a][:, lo:hi].bitcast(FP8X4),
+                    rhs_scale=v_plane[4 * a : P, lo:hi],
+                    start=(a == 0),
+                    stop=(a == 1),
+                )
+            nc.scalar.activation(out=val, in_=acc, func=ACT.Identity, bias=b1_sb[:, t : t + 1], scale=1.0)
+
+        def short_unit(n, t, lo, hi, h):
+            w = hi - lo
+            val = work.tile([P, w], F32, name="short_val")
+            product(t, lo, hi, banks[6 + n][:, :w], val[:])
+            whole = work.tile([P, w], I32, name="short_whole")
+            nc.vector.tensor_scalar(whole[:], val[:], 1.0 / TURN, 1.0, ALU.mult, ALU.add)
+            red = work.tile([P, w], F32, name="short_red")
+            nc.vector.scalar_tensor_tensor(out=red[:], in0=whole[:], scalar=-TURN, in1=val[:], op0=ALU.mult, op1=ALU.add)
+            mag = work.tile([P, w], F32, name="short_mag")
+            nc.scalar.activation(out=mag[:], in_=red[:], func=ACT.Abs, bias=TURN, scale=1.0)
+            cosv = work.tile([P, w], F32, name="short_cos")
+            nc.scalar.activation(out=cosv[:], in_=mag[:], func=ACT.Sin, bias=math.pi / 2, scale=-1.0)
+            nc.vector.scalar_tensor_tensor(
+                out=h[:, lo:hi], in0=cosv[:], scalar=gain_sb[:, t : t + 1], in1=val[:], op0=ALU.mult, op1=ALU.mult
+            )
+
+        def long_unit(n, t, lo, hi, h):
+            val = vals[n % RING]
+            red = banks[2 + n % 2]
+            cosv = banks[4 + n % 4]
+            product(t, lo, hi, banks[n % 2][:], val[:])
+            turns = work.tile([P, BANK], U32, name="turns")
+            nc.scalar.activation(out=turns[:], in_=val[:], func=ACT.Copy, bias=TURN_SHIFT, scale=1.0 / TURN)
+            back = work.tile([P, BANK], F32, name="back")
+            nc.scalar.activation(out=back[:], in_=turns[:], func=ACT.Copy, bias=TURN * TURN_SHIFT, scale=-TURN)
+            for c in range(0, BANK, P):
+                nc.tensor.matmul(red[:, c : c + P], val[:, c : c + P], ident[:], start=True, stop=False, is_transpose=True)
+                nc.tensor.matmul(red[:, c : c + P], back[:, c : c + P], ident[:], start=False, stop=True, is_transpose=True)
+            mag = work.tile([P, BANK], F32, name="mag")
+            nc.scalar.activation(out=mag[:], in_=red[:], func=ACT.Abs)
+            cos_t = work.tile([P, BANK], F32, name="cos_t")
+            nc.scalar.activation(out=cos_t[:], in_=mag[:], func=ACT.Sin, bias=math.pi / 2, scale=-1.0)
+            for c in range(0, BANK, P):
+                nc.tensor.transpose(cosv[:, c : c + P], cos_t[:, c : c + P], ident[:])
+            nc.vector.scalar_tensor_tensor(
+                out=h[:, lo:hi], in0=cosv[:], scalar=gain_sb[:, t : t + 1], in1=val[:], op0=ALU.mult, op1=ALU.mult
+            )
+
+        for t in range(PACK):
+            h = work.tile([P, S], F32, name="h", tag="wide")
+            if t == 0:
+                for n, (lo, hi) in enumerate(J_PIECES):
+                    if hi - lo < BANK:
+                        short_unit(n, t, lo, hi, h)
+                    else:
+                        long_unit(0, t, lo, hi, h)
+                    nc.vector.tensor_tensor(
+                        page[t][:].indirect(idx2[:, lo // 16 : hi // 16]), h[:, lo:hi], wgs_first[:, lo:hi], ALU.mult
+                    )
+            else:
+                for lo in range(0, S, BANK):
+                    long_unit(2 * t - 1 + lo // BANK, t, lo, lo + BANK, h)
+                nc.vector.tensor_tensor(page[t][:].indirect(idx2[:]), h[:], wgs_rest[:, t - 1, :], ALU.mult)
+
+        count = []
+        w5_bf = keep.tile([P, PACK * N], BF16, name="w5_bf", tag="v_codes0", align_bytes=64)
+        w5_codes = keep.tile([P, N], U32, name="w5_codes", align_bytes=64)
+        w5_plane = keep.tile([P, N], U8, name="w5_plane", align_bytes=64)
+        nc.scalar.copy(
+            out=w5_bf[:].rearrange("p (c e i) -> p c i e", e=4, i=PACK),
+            in_=w5_raw[:].rearrange("p i (c e) -> p c i e", e=4),
+        )
+        nc.vector.quantize_mx(out=w5_codes[:].bitcast(FP8X4), scales=w5_plane[:], in_=w5_bf[:])
+
+        out_rows = out.rearrange("(b p) m -> p b m", p=P)
+        for lo, hi in M_PIECES:
+            w = hi - lo
+            x = work.tile([P, PACK, w], F32, name="x", tag="wide")
+            for t in range(PACK):
+                nc.vector.tensor_tensor(
+                    x[:, t, :], page[t][:].indirect(idx3[:, lo // 16 : hi // 16]), wgt_sb[:, lo:hi], ALU.mult
+                )
+            x_bf = work.tile([P, PACK * w], BF16, name="x_bf", align_bytes=64)
+            nc.scalar.copy(
+                out=x_bf[:].rearrange("p (c e i) -> p c i e", e=4, i=PACK),
+                in_=x[:].rearrange("p i (c e) -> p c i e", e=4),
+            )
+            x_codes = work.tile([P, w], U32, name="x_codes", align_bytes=64)
+            x_plane = work.tile([P, w], U8, name="x_plane", align_bytes=64)
+            nc.vector.quantize_mx(out=x_codes[:].bitcast(FP8X4), scales=x_plane[:], in_=x_bf[:])
+            per_bank = BANK // w
+            for b0 in range(0, N // P, per_bank):
+                y1 = banks[2 * (len(count) % 4)]
+                y2 = banks[2 * (len(count) % 4) + 1]
+                count.append(b0)
+                for s in range(per_bank):
+                    b = b0 + s
+                    nc.tensor.matmul_mx(
+                        out=y1[:, s * w : (s + 1) * w],
+                        lhsT=w4_codes[:, 2 * P * b : 2 * P * (b + 1)].bitcast(FP4X4),
+                        lhsT_scale=w4_plane[:, P * b : P * (b + 1)],
+                        rhs=x_codes[:].bitcast(FP8X4),
+                        rhs_scale=x_plane[:],
+                        start=True,
+                        stop=True,
+                    )
+                for s in range(per_bank):
+                    b = b0 + s
+                    nc.tensor.matmul_mx(
+                        out=y2[:, s * w : (s + 1) * w],
+                        lhsT=w5_codes[:, P * b : P * (b + 1)].bitcast(FP8X4),
+                        lhsT_scale=w5_plane[:, P * b : P * (b + 1)],
+                        rhs=x_codes[:].bitcast(FP8X4),
+                        rhs_scale=x_plane[:],
+                        start=True,
+                        stop=True,
+                    )
+                y1_sb = work.tile([P, BANK], F32, name="y1_sb")
+                nc.scalar.copy(out=y1_sb[:], in_=y1[:])
+                res = work.tile([P, BANK], F32, name="res", bufs=4)
+                nc.vector.tensor_tensor(res[:], y2[:], y1_sb[:], ALU.max)
+                nc.sync.dma_start(
+                    out=out_rows[:, b0 : b0 + per_bank, lo:hi], in_=res[:].rearrange("p (s m) -> p s m", s=per_bank)
+                )

@@ -24,7 +24,7 @@ BANK = 512
 TURN = 2.0 * math.pi
 TURN_SHIFT = 65536.0
 RING = 5
-J_PIECES = [(0, 256), (256, 512), (512, 1024)]
+PIECE = 256
 M_PIECES = [(0, 256), (256, 512), (512, 768), (768, 896), (896, 1024)]
 
 
@@ -35,6 +35,7 @@ def tile_list_drowsiness_warning_features_kernel(
     with ExitStack() as ctx:
         lists = ctx.enter_context(tc.tile_pool(name="lists", bufs=1))
         keep = ctx.enter_context(tc.tile_pool(name="keep", bufs=1))
+        head = ctx.enter_context(tc.tile_pool(name="head", bufs=1))
         work = ctx.enter_context(tc.tile_pool(name="work", bufs=2))
         psum = ctx.enter_context(tc.psum_pool(name="psum", bufs=1))
 
@@ -46,6 +47,9 @@ def tile_list_drowsiness_warning_features_kernel(
         nc.vector.memset(tab_plane[:].bitcast(I32), 0)
         w4_plane = keep.tile([P, N], U8, name="w4_plane", align_bytes=64)
         nc.gpsimd.memset(w4_plane[:].bitcast(I32), 0)
+        warm = keep.tile([P, 8], F32, name="warm")
+        nc.gpsimd.memset(warm[:], 0.0)
+        nc.scalar.activation(out=warm[:, 1:2], in_=warm[:, 0:1], func=ACT.Sin)
         ident = keep.tile([P, P], F32, name="ident")
         make_identity(nc, ident[:])
 
@@ -92,97 +96,107 @@ def tile_list_drowsiness_warning_features_kernel(
                 out=w4_plane[32 * q : 32 * q + 4, :].bitcast(I32), in_=w4_scales[0, 4 * q : 4 * q + 4, :].bitcast(I32)
             )
 
-        w1_bf = [keep.tile([P, PACK * H], BF16, name=f"w1_bf{a}", align_bytes=64) for a in range(2)]
+        w1_bf = [head.tile([P, PACK * H], BF16, name=f"w1_bf{a}", align_bytes=64, offset=4096 * a) for a in range(2)]
         w1_codes = [keep.tile([P, H], U32, name=f"w1_codes{a}", align_bytes=64) for a in range(2)]
         w1_plane = [keep.tile([P, H], U8, name=f"w1_plane{a}", align_bytes=64) for a in range(2)]
-        dealt = [w1_bf[a][:].rearrange("p (t m i) -> p m t i", t=PACK, i=PACK) for a in range(2)]
-        raw = [w1_raw[a][:].rearrange("p i (m t) -> p m t i", t=PACK) for a in range(2)]
-        nc.scalar.copy(out=dealt[0], in_=raw[0])
-        nc.vector.tensor_copy(out=dealt[1][:, 0:64], in_=raw[1][:, 0:64])
-        nc.scalar.copy(out=dealt[1][:, 64:128], in_=raw[1][:, 64:128])
-
-        v_codes = [keep.tile([P, S], U32, name=f"v_codes{a}", align_bytes=64) for a in range(2)]
         v_plane = keep.tile([P, S], U8, name="v_plane", align_bytes=64)
-        for lo, hi in J_PIECES:
-            nc.vector.tensor_copy(v_plane[:, lo:hi], tab_plane[:].indirect(idx[:, lo // 16 : hi // 16]))
+        nc.vector.tensor_copy(v_plane[:], tab_plane[:].indirect(idx[:]))
         for a in range(2):
+            nc.scalar.copy(
+                out=w1_bf[a][:].rearrange("p (t m i) -> p m t i", t=PACK, i=PACK),
+                in_=w1_raw[a][:].rearrange("p i (m t) -> p m t i", t=PACK),
+            )
             nc.vector.quantize_mx(out=w1_codes[a][:].bitcast(FP8X4), scales=w1_plane[a][:], in_=w1_bf[a][:])
-        for lo, hi in J_PIECES:
-            for a in range(2):
-                nc.vector.tensor_copy(v_codes[a][:, lo:hi], tab[a][:].bitcast(U32).indirect(idx[:, lo // 16 : hi // 16]))
+
+        places = {(0, 0): 0, (0, 1): 1024, (1, 0): 4096, (1, 1): 5120, (0, 2): 6144, (1, 2): 7168, (0, 3): 8192, (1, 3): 9216}
+        picked = {}
+
+        def pick(a, c):
+            tile = head.tile([P, PIECE], U32, name=f"picked{a}{c}", align_bytes=64, offset=places[(a, c)])
+            nc.vector.tensor_copy(tile[:], tab[a][:].bitcast(U32).indirect(idx[:, c * PIECE // 16 : (c + 1) * PIECE // 16]))
+            picked.setdefault((a, c), tile)
+
+        for a, c in [(0, 0), (0, 1), (1, 0), (1, 1), (0, 2), (1, 2)]:
+            pick(a, c)
 
         banks = [psum.tile([P, BANK], F32, name=f"bank{i}") for i in range(8)]
         vals = [keep.tile([P, BANK], F32, name=f"val{i}") for i in range(RING)]
 
         def product(t, lo, hi, acc, val):
-            for a in range(2):
-                nc.tensor.matmul_mx(
-                    out=acc,
-                    lhsT=w1_codes[a][:, P * t : P * (t + 1)].bitcast(FP8X4),
-                    lhsT_scale=w1_plane[a][:, P * t : P * (t + 1)],
-                    rhs=v_codes[a][:, lo:hi].bitcast(FP8X4),
-                    rhs_scale=v_plane[4 * a : P, lo:hi],
-                    start=(a == 0),
-                    stop=(a == 1),
-                )
+            for c in range(lo // PIECE, hi // PIECE):
+                for a in range(2):
+                    nc.tensor.matmul_mx(
+                        out=acc[:, c * PIECE - lo : (c + 1) * PIECE - lo],
+                        lhsT=w1_codes[a][:, P * t : P * (t + 1)].bitcast(FP8X4),
+                        lhsT_scale=w1_plane[a][:, P * t : P * (t + 1)],
+                        rhs=picked[(a, c)][:].bitcast(FP8X4),
+                        rhs_scale=v_plane[4 * a : P, c * PIECE : (c + 1) * PIECE],
+                        start=(a == 0),
+                        stop=(a == 1),
+                    )
             nc.scalar.activation(out=val, in_=acc, func=ACT.Identity, bias=b1_sb[:, t : t + 1], scale=1.0)
 
-        def short_unit(n, t, lo, hi, h):
-            w = hi - lo
-            val = work.tile([P, w], F32, name="short_val")
-            product(t, lo, hi, banks[6 + n][:, :w], val[:])
-            whole = work.tile([P, w], I32, name="short_whole")
-            nc.vector.tensor_scalar(whole[:], val[:], 1.0 / TURN, 1.0, ALU.mult, ALU.add)
-            red = work.tile([P, w], F32, name="short_red")
+        def scatter(t, lo, hi, h, weights):
+            nc.vector.tensor_tensor(page[t][:].indirect(idx2[:, lo // 16 : hi // 16]), h[:, lo:hi], weights, ALU.mult)
+
+        def short_front(n):
+            val = work.tile([P, PIECE], F32, name="short_val", bufs=4)
+            product(0, n * PIECE, (n + 1) * PIECE, banks[4 + n][:, :PIECE], val[:])
+            whole = head.tile([P, PIECE], I32, name=f"whole{n}", align_bytes=64, offset=8704 if n == 0 else 9216 + 1024 * n)
+            nc.vector.tensor_scalar(whole[:], val[:], 1.0 / TURN, None, ALU.mult)
+            red = work.tile([P, PIECE], F32, name="short_red", bufs=4)
             nc.vector.scalar_tensor_tensor(out=red[:], in0=whole[:], scalar=-TURN, in1=val[:], op0=ALU.mult, op1=ALU.add)
-            mag = work.tile([P, w], F32, name="short_mag")
-            nc.scalar.activation(out=mag[:], in_=red[:], func=ACT.Abs, bias=TURN, scale=1.0)
-            cosv = work.tile([P, w], F32, name="short_cos")
+            return val, red
+
+        def short_back(n, val, red, h):
+            mag = work.tile([P, PIECE], F32, name="short_mag")
+            nc.scalar.activation(out=mag[:], in_=red[:], func=ACT.Abs)
+            cosv = work.tile([P, PIECE], F32, name="short_cos")
             nc.scalar.activation(out=cosv[:], in_=mag[:], func=ACT.Sin, bias=math.pi / 2, scale=-1.0)
             nc.vector.scalar_tensor_tensor(
-                out=h[:, lo:hi], in0=cosv[:], scalar=gain_sb[:, t : t + 1], in1=val[:], op0=ALU.mult, op1=ALU.mult
+                out=h[:, n * PIECE : (n + 1) * PIECE], in0=cosv[:], scalar=gain_sb[:, 0:1], in1=val[:], op0=ALU.mult, op1=ALU.mult
             )
 
         def long_unit(n, t, lo, hi, h):
-            val = vals[n % RING]
+            w = hi - lo
+            val = vals[n % RING][:, :w]
             red = banks[2 + n % 2]
             cosv = banks[4 + n % 4]
-            product(t, lo, hi, banks[n % 2][:], val[:])
-            turns = work.tile([P, BANK], U32, name="turns")
-            nc.scalar.activation(out=turns[:], in_=val[:], func=ACT.Copy, bias=TURN_SHIFT, scale=1.0 / TURN)
-            back = work.tile([P, BANK], F32, name="back")
+            product(t, lo, hi, banks[n % 2][:, :w], val)
+            turns = work.tile([P, w], U32, name="turns")
+            nc.scalar.activation(out=turns[:], in_=val, func=ACT.Copy, bias=TURN_SHIFT, scale=1.0 / TURN)
+            back = work.tile([P, w], F32, name="back")
             nc.scalar.activation(out=back[:], in_=turns[:], func=ACT.Copy, bias=TURN * TURN_SHIFT, scale=-TURN)
-            for c in range(0, BANK, P):
+            for c in range(0, w, P):
                 nc.tensor.matmul(red[:, c : c + P], val[:, c : c + P], ident[:], start=True, stop=False, is_transpose=True)
                 nc.tensor.matmul(red[:, c : c + P], back[:, c : c + P], ident[:], start=False, stop=True, is_transpose=True)
-            mag = work.tile([P, BANK], F32, name="mag")
-            nc.scalar.activation(out=mag[:], in_=red[:], func=ACT.Abs)
-            cos_t = work.tile([P, BANK], F32, name="cos_t")
+            mag = work.tile([P, w], F32, name="mag")
+            nc.scalar.activation(out=mag[:], in_=red[:, :w], func=ACT.Abs)
+            cos_t = work.tile([P, w], F32, name="cos_t")
             nc.scalar.activation(out=cos_t[:], in_=mag[:], func=ACT.Sin, bias=math.pi / 2, scale=-1.0)
-            for c in range(0, BANK, P):
+            for c in range(0, w, P):
                 nc.tensor.transpose(cosv[:, c : c + P], cos_t[:, c : c + P], ident[:])
             nc.vector.scalar_tensor_tensor(
-                out=h[:, lo:hi], in0=cosv[:], scalar=gain_sb[:, t : t + 1], in1=val[:], op0=ALU.mult, op1=ALU.mult
+                out=h[:, lo:hi], in0=cosv[:, :w], scalar=gain_sb[:, t : t + 1], in1=val, op0=ALU.mult, op1=ALU.mult
             )
 
-        for t in range(PACK):
+        h = work.tile([P, S], F32, name="h", tag="wide")
+        fronts = [short_front(0)]
+        pick(0, 3)
+        pick(1, 3)
+        fronts.extend([short_front(n) for n in range(1, S // PIECE)])
+        for n, (val, red) in enumerate(fronts):
+            short_back(n, val, red, h)
+            lo = n * PIECE
+            scatter(0, lo, lo + PIECE, h, wgs_first[:, lo : lo + PIECE])
+        for t in range(1, PACK):
             h = work.tile([P, S], F32, name="h", tag="wide")
-            if t == 0:
-                for n, (lo, hi) in enumerate(J_PIECES):
-                    if hi - lo < BANK:
-                        short_unit(n, t, lo, hi, h)
-                    else:
-                        long_unit(0, t, lo, hi, h)
-                    nc.vector.tensor_tensor(
-                        page[t][:].indirect(idx2[:, lo // 16 : hi // 16]), h[:, lo:hi], wgs_first[:, lo:hi], ALU.mult
-                    )
-            else:
-                for lo in range(0, S, BANK):
-                    long_unit(2 * t - 1 + lo // BANK, t, lo, lo + BANK, h)
-                nc.vector.tensor_tensor(page[t][:].indirect(idx2[:]), h[:], wgs_rest[:, t - 1, :], ALU.mult)
+            for lo in range(0, S, BANK):
+                long_unit(2 * (t - 1) + lo // BANK, t, lo, lo + BANK, h)
+                scatter(t, lo, lo + BANK, h, wgs_rest[:, t - 1, lo : lo + BANK])
 
         count = []
-        w5_bf = keep.tile([P, PACK * N], BF16, name="w5_bf", tag="v_codes0", align_bytes=64)
+        w5_bf = head.tile([P, PACK * N], BF16, name="w5_bf", align_bytes=64, offset=0)
         w5_codes = keep.tile([P, N], U32, name="w5_codes", align_bytes=64)
         w5_plane = keep.tile([P, N], U8, name="w5_plane", align_bytes=64)
         nc.scalar.copy(

@@ -24,7 +24,7 @@ BANK = 512
 TURN = 2.0 * math.pi
 TURN_SHIFT = 65536.0
 RING = 5
-PIECE = 256
+J_PIECES = [(0, 256), (256, 512), (512, 1024)]
 M_PIECES = [(0, 256), (256, 512), (512, 768), (768, 896), (896, 1024)]
 
 
@@ -62,10 +62,10 @@ def tile_list_drowsiness_warning_features_kernel(
                 out=tab_plane[32 * q : 32 * q + 8, :].bitcast(I32),
                 in_=tab_scales[:, 4 * q : 4 * q + 4, :].bitcast(I32),
             )
-        nc.sync.dma_start(out=w1_raw[1][:], in_=w1_rows[1])
         tab = [keep.tile([P, T], I32, name=f"tab{a}") for a in range(2)]
-        for a in range(2):
-            nc.sync.dma_start(out=tab[a][:], in_=tab_words[a].rearrange("p t i -> p (t i)").bitcast(I32))
+        nc.sync.dma_start(out=tab[0][:], in_=tab_words[0].rearrange("p t i -> p (t i)").bitcast(I32))
+        nc.sync.dma_start(out=w1_raw[1][:], in_=w1_rows[1])
+        nc.sync.dma_start(out=tab[1][:], in_=tab_words[1].rearrange("p t i -> p (t i)").bitcast(I32))
         b1_sb = keep.tile([P, PACK], F32, name="b1_sb")
         gain_sb = keep.tile([P, PACK], F32, name="gain_sb")
         nc.sync.dma_start(out=b1_sb[:], in_=b1.rearrange("(p i) -> p i", i=PACK))
@@ -96,65 +96,64 @@ def tile_list_drowsiness_warning_features_kernel(
                 out=w4_plane[32 * q : 32 * q + 4, :].bitcast(I32), in_=w4_scales[0, 4 * q : 4 * q + 4, :].bitcast(I32)
             )
 
-        w1_bf = [head.tile([P, PACK * H], BF16, name=f"w1_bf{a}", align_bytes=64, offset=4096 * a) for a in range(2)]
         w1_codes = [keep.tile([P, H], U32, name=f"w1_codes{a}", align_bytes=64) for a in range(2)]
         w1_plane = [keep.tile([P, H], U8, name=f"w1_plane{a}", align_bytes=64) for a in range(2)]
+
+        def quantise_w1(a, t0, t1, place):
+            rounded = head.tile([P, (t1 - t0) * P * PACK], BF16, name=f"w1_bf{a}{t0}", align_bytes=64, offset=place)
+            nc.scalar.copy(
+                out=rounded[:].rearrange("p (t m i) -> p m t i", m=P, i=PACK),
+                in_=w1_raw[a][:].rearrange("p i (m t) -> p m t i", t=PACK)[:, :, t0:t1, :],
+            )
+            cols = slice(P * t0, P * t1)
+            nc.vector.quantize_mx(out=w1_codes[a][:, cols].bitcast(FP8X4), scales=w1_plane[a][:, cols], in_=rounded[:])
+
+        def pick(dst, a, lo, hi):
+            nc.vector.tensor_copy(dst[:, lo:hi], tab[a][:].bitcast(U32).indirect(idx[:, lo // 16 : hi // 16]))
+
         v_plane = keep.tile([P, S], U8, name="v_plane", align_bytes=64)
         nc.vector.tensor_copy(v_plane[:], tab_plane[:].indirect(idx[:]))
-        for a in range(2):
-            nc.scalar.copy(
-                out=w1_bf[a][:].rearrange("p (t m i) -> p m t i", t=PACK, i=PACK),
-                in_=w1_raw[a][:].rearrange("p i (m t) -> p m t i", t=PACK),
-            )
-            nc.vector.quantize_mx(out=w1_codes[a][:].bitcast(FP8X4), scales=w1_plane[a][:], in_=w1_bf[a][:])
-
-        places = {(0, 0): 0, (0, 1): 1024, (1, 0): 4096, (1, 1): 5120, (0, 2): 6144, (1, 2): 7168, (0, 3): 8192, (1, 3): 9216}
-        picked = {}
-
-        def pick(a, c):
-            tile = head.tile([P, PIECE], U32, name=f"picked{a}{c}", align_bytes=64, offset=places[(a, c)])
-            nc.vector.tensor_copy(tile[:], tab[a][:].bitcast(U32).indirect(idx[:, c * PIECE // 16 : (c + 1) * PIECE // 16]))
-            picked.setdefault((a, c), tile)
-
-        for a, c in [(0, 0), (0, 1), (1, 0), (1, 1), (0, 2), (1, 2)]:
-            pick(a, c)
+        quantise_w1(0, 0, 4, 0)
+        v_codes = [head.tile([P, S], U32, name=f"v_codes{a}", align_bytes=64, offset=4096 * a) for a in range(2)]
+        pick(v_codes[0], 0, 0, S)
+        quantise_w1(1, 0, 2, 4096)
+        quantise_w1(1, 2, 4, 8192)
+        for lo, hi in J_PIECES:
+            pick(v_codes[1], 1, lo, hi)
 
         banks = [psum.tile([P, BANK], F32, name=f"bank{i}") for i in range(8)]
         vals = [keep.tile([P, BANK], F32, name=f"val{i}") for i in range(RING)]
 
         def product(t, lo, hi, acc, val):
-            for c in range(lo // PIECE, hi // PIECE):
-                for a in range(2):
-                    nc.tensor.matmul_mx(
-                        out=acc[:, c * PIECE - lo : (c + 1) * PIECE - lo],
-                        lhsT=w1_codes[a][:, P * t : P * (t + 1)].bitcast(FP8X4),
-                        lhsT_scale=w1_plane[a][:, P * t : P * (t + 1)],
-                        rhs=picked[(a, c)][:].bitcast(FP8X4),
-                        rhs_scale=v_plane[4 * a : P, c * PIECE : (c + 1) * PIECE],
-                        start=(a == 0),
-                        stop=(a == 1),
-                    )
+            for a in range(2):
+                nc.tensor.matmul_mx(
+                    out=acc,
+                    lhsT=w1_codes[a][:, P * t : P * (t + 1)].bitcast(FP8X4),
+                    lhsT_scale=w1_plane[a][:, P * t : P * (t + 1)],
+                    rhs=v_codes[a][:, lo:hi].bitcast(FP8X4),
+                    rhs_scale=v_plane[4 * a : P, lo:hi],
+                    start=(a == 0),
+                    stop=(a == 1),
+                )
             nc.scalar.activation(out=val, in_=acc, func=ACT.Identity, bias=b1_sb[:, t : t + 1], scale=1.0)
 
         def scatter(t, lo, hi, h, weights):
             nc.vector.tensor_tensor(page[t][:].indirect(idx2[:, lo // 16 : hi // 16]), h[:, lo:hi], weights, ALU.mult)
 
-        def short_front(n):
-            val = work.tile([P, PIECE], F32, name="short_val", bufs=4)
-            product(0, n * PIECE, (n + 1) * PIECE, banks[4 + n][:, :PIECE], val[:])
-            whole = head.tile([P, PIECE], I32, name=f"whole{n}", align_bytes=64, offset=8704 if n == 0 else 9216 + 1024 * n)
+        def short_unit(n, lo, hi, h):
+            w = hi - lo
+            val = work.tile([P, w], F32, name="short_val", bufs=3)
+            product(0, lo, hi, banks[4 + n][:, :w], val[:])
+            whole = work.tile([P, w], I32, name="whole")
             nc.vector.tensor_scalar(whole[:], val[:], 1.0 / TURN, None, ALU.mult)
-            red = work.tile([P, PIECE], F32, name="short_red", bufs=4)
+            red = work.tile([P, w], F32, name="short_red", bufs=3)
             nc.vector.scalar_tensor_tensor(out=red[:], in0=whole[:], scalar=-TURN, in1=val[:], op0=ALU.mult, op1=ALU.add)
-            return val, red
-
-        def short_back(n, val, red, h):
-            mag = work.tile([P, PIECE], F32, name="short_mag")
+            mag = work.tile([P, w], F32, name="mag")
             nc.scalar.activation(out=mag[:], in_=red[:], func=ACT.Abs)
-            cosv = work.tile([P, PIECE], F32, name="short_cos")
+            cosv = work.tile([P, w], F32, name="short_cos", bufs=3)
             nc.scalar.activation(out=cosv[:], in_=mag[:], func=ACT.Sin, bias=math.pi / 2, scale=-1.0)
             nc.vector.scalar_tensor_tensor(
-                out=h[:, n * PIECE : (n + 1) * PIECE], in0=cosv[:], scalar=gain_sb[:, 0:1], in1=val[:], op0=ALU.mult, op1=ALU.mult
+                out=h[:, lo:hi], in0=cosv[:], scalar=gain_sb[:, 0:1], in1=val[:], op0=ALU.mult, op1=ALU.mult
             )
 
         def long_unit(n, t, lo, hi, h):
@@ -181,19 +180,17 @@ def tile_list_drowsiness_warning_features_kernel(
             )
 
         h = work.tile([P, S], F32, name="h", tag="wide")
-        fronts = [short_front(0)]
-        pick(0, 3)
-        pick(1, 3)
-        fronts.extend([short_front(n) for n in range(1, S // PIECE)])
-        for n, (val, red) in enumerate(fronts):
-            short_back(n, val, red, h)
-            lo = n * PIECE
-            scatter(0, lo, lo + PIECE, h, wgs_first[:, lo : lo + PIECE])
+        for n, (lo, hi) in enumerate(J_PIECES):
+            short_unit(n, lo, hi, h)
+            scatter(0, lo, hi, h, wgs_first[:, lo:hi])
         for t in range(1, PACK):
             h = work.tile([P, S], F32, name="h", tag="wide")
             for lo in range(0, S, BANK):
                 long_unit(2 * (t - 1) + lo // BANK, t, lo, lo + BANK, h)
-                scatter(t, lo, lo + BANK, h, wgs_rest[:, t - 1, lo : lo + BANK])
+                if t == 1:
+                    scatter(t, lo, lo + BANK, h, wgs_rest[:, t - 1, lo : lo + BANK])
+            if t > 1:
+                scatter(t, 0, S, h, wgs_rest[:, t - 1, :])
 
         count = []
         w5_bf = head.tile([P, PACK * N], BF16, name="w5_bf", align_bytes=64, offset=0)

import math
from contextlib import ExitStack

import concourse.mybir as mybir
from concourse.masks import make_identity

K, T, S, T2, M, H, N = 1024, 2048, 1024, 2048, 1024, 512, 512
FLOPS = 2 * K * H * S + 2 * 2 * H * N * M

F32 = mybir.dt.float32
BF16 = mybir.dt.bfloat16
I32 = mybir.dt.int32
U32 = mybir.dt.uint32
U16 = mybir.dt.uint16
U8 = mybir.dt.uint8
FP8X4 = mybir.dt.float8_e4m3fn_x4
FP4X4 = mybir.dt.float4_e2m1fn_x4
ACT = mybir.ActivationFunctionType
ALU = mybir.AluOpType

P = 128
PACK = 4
BANK = 512
TURN = 2.0 * math.pi
TURN_SHIFT = 65536.0
RING = 5
J_PIECES = [(0, 256), (256, 512), (512, 1024)]
M_PIECES = [(0, 256), (256, 512), (512, 768), (768, 896), (896, 1024)]


def tile_list_drowsiness_warning_features_kernel(
    tc, tab_words, tab_scales, offs, w1, b1, gain, page0, wgs, offs2, wgt, offs3, w4_words, w4_scales, w5, out
):
    nc = tc.nc
    with ExitStack() as ctx:
        lists = ctx.enter_context(tc.tile_pool(name="lists", bufs=1))
        keep = ctx.enter_context(tc.tile_pool(name="keep", bufs=1))
        head = ctx.enter_context(tc.tile_pool(name="head", bufs=1))
        work = ctx.enter_context(tc.tile_pool(name="work", bufs=2))
        psum = ctx.enter_context(tc.psum_pool(name="psum", bufs=1))

        idx = lists.tile([P, S // 16], U16, name="idx")
        idx2 = lists.tile([P, S // 16], U16, name="idx2")
        idx3 = lists.tile([P, M // 16], U16, name="idx3")

        tab_plane = keep.tile([P, T], U8, name="tab_plane")
        nc.vector.memset(tab_plane[:].bitcast(I32), 0)
        w4_plane = keep.tile([P, N], U8, name="w4_plane", align_bytes=64)
        nc.gpsimd.memset(w4_plane[:].bitcast(I32), 0)
        warm = keep.tile([P, 8], F32, name="warm")
        nc.gpsimd.memset(warm[:], 0.0)
        nc.scalar.activation(out=warm[:, 1:2], in_=warm[:, 0:1], func=ACT.Sin)
        ident = keep.tile([P, P], F32, name="ident")
        make_identity(nc, ident[:])

        w1_raw = [keep.tile([P, PACK, H], F32, name=f"w1_raw{a}") for a in range(2)]
        w1_rows = w1.rearrange("(a p i) r -> a p i r", a=2, i=PACK)
        nc.sync.dma_start(idx[:], offs)
        nc.sync.dma_start(out=w1_raw[0][:], in_=w1_rows[0])
        for q in range(4):
            nc.sync.dma_start(
                out=tab_plane[32 * q : 32 * q + 8, :].bitcast(I32),
                in_=tab_scales[:, 4 * q : 4 * q + 4, :].bitcast(I32),
            )
        tab = [keep.tile([P, T], I32, name=f"tab{a}") for a in range(2)]
        nc.sync.dma_start(out=tab[0][:], in_=tab_words[0].rearrange("p t i -> p (t i)").bitcast(I32))
        nc.sync.dma_start(out=w1_raw[1][:], in_=w1_rows[1])
        nc.sync.dma_start(out=tab[1][:], in_=tab_words[1].rearrange("p t i -> p (t i)").bitcast(I32))
        b1_sb = keep.tile([P, PACK], F32, name="b1_sb")
        gain_sb = keep.tile([P, PACK], F32, name="gain_sb")
        nc.sync.dma_start(out=b1_sb[:], in_=b1.rearrange("(p i) -> p i", i=PACK))
        nc.sync.dma_start(out=gain_sb[:], in_=gain.rearrange("(p i) -> p i", i=PACK))
        nc.sync.dma_start(idx2[:], offs2)
        page = [keep.tile([P, T2], F32, name=f"page{i}") for i in range(PACK)]
        page_rows = page0.rearrange("(p i) c -> p i c", i=PACK)
        wgs_rows = wgs.rearrange("(s i) j -> s i j", i=PACK)
        wgs_first = keep.tile([P, S], F32, name="wgs_first")
        wgs_rest = keep.tile([P, PACK - 1, S], F32, name="wgs_rest")
        nc.sync.dma_start(out=page[0][:], in_=page_rows[:, 0, :])
        for q in (0, 2, 1, 3):
            nc.sync.dma_start(out=wgs_first[32 * q : 32 * q + 32, :], in_=wgs_rows[:, 0, :])
        nc.sync.dma_start(out=page[1][:], in_=page_rows[:, 1, :])
        for q in (0, 2, 1, 3):
            nc.sync.dma_start(out=wgs_rest[32 * q : 32 * q + 32, :, :], in_=wgs_rows[:, 1:, :])
        nc.sync.dma_start(out=page[2][:], in_=page_rows[:, 2, :])
        nc.sync.dma_start(out=page[3][:], in_=page_rows[:, 3, :])
        w5_raw = keep.tile([P, PACK, N], F32, name="w5_raw")
        nc.sync.dma_start(out=w5_raw[:], in_=w5.rearrange("(p i) n -> p i n", i=PACK))
        wgt_sb = keep.tile([P, M], F32, name="wgt_sb")
        nc.sync.dma_start(out=wgt_sb[:], in_=wgt)
        nc.sync.dma_start(idx3[:], offs3)
        w4_codes = keep.tile([P, 2 * N], U8, name="w4_codes", align_bytes=64)
        nc.sync.dma_start(out=w4_codes[:].bitcast(I32), in_=w4_words[0].bitcast(I32))
        for q in range(4):
            nc.sync.dma_start(
                out=w4_plane[32 * q : 32 * q + 4, :].bitcast(I32), in_=w4_scales[0, 4 * q : 4 * q + 4, :].bitcast(I32)
            )

        w1_codes = [keep.tile([P, H], U32, name=f"w1_codes{a}", align_bytes=64) for a in range(2)]
        w1_plane = [keep.tile([P, H], U8, name=f"w1_plane{a}", align_bytes=64) for a in range(2)]

        def quantise_w1(a, t0, t1, place):
            rounded = head.tile([P, (t1 - t0) * P * PACK], BF16, name=f"w1_bf{a}{t0}", align_bytes=64, offset=place)
            nc.scalar.copy(
                out=rounded[:].rearrange("p (t m i) -> p m t i", m=P, i=PACK),
                in_=w1_raw[a][:].rearrange("p i (m t) -> p m t i", t=PACK)[:, :, t0:t1, :],
            )
            cols = slice(P * t0, P * t1)
            nc.vector.quantize_mx(out=w1_codes[a][:, cols].bitcast(FP8X4), scales=w1_plane[a][:, cols], in_=rounded[:])

        def pick(dst, a, lo, hi):
            nc.vector.tensor_copy(dst[:, lo:hi], tab[a][:].bitcast(U32).indirect(idx[:, lo // 16 : hi // 16]))

        v_plane = keep.tile([P, S], U8, name="v_plane", align_bytes=64)
        nc.vector.tensor_copy(v_plane[:], tab_plane[:].indirect(idx[:]))
        quantise_w1(0, 0, 4, 0)
        v_codes = [head.tile([P, S], U32, name=f"v_codes{a}", align_bytes=64, offset=4096 * a) for a in range(2)]
        pick(v_codes[0], 0, 0, S)
        quantise_w1(1, 0, 2, 4096)
        quantise_w1(1, 2, 4, 8192)
        for lo, hi in J_PIECES:
            pick(v_codes[1], 1, lo, hi)

        banks = [psum.tile([P, BANK], F32, name=f"bank{i}") for i in range(8)]
        vals = [keep.tile([P, BANK], F32, name=f"val{i}") for i in range(RING)]

        def product(t, lo, hi, acc, val):
            for a in range(2):
                nc.tensor.matmul_mx(
                    out=acc,
                    lhsT=w1_codes[a][:, P * t : P * (t + 1)].bitcast(FP8X4),
                    lhsT_scale=w1_plane[a][:, P * t : P * (t + 1)],
                    rhs=v_codes[a][:, lo:hi].bitcast(FP8X4),
                    rhs_scale=v_plane[4 * a : P, lo:hi],
                    start=(a == 0),
                    stop=(a == 1),
                )
            nc.scalar.activation(out=val, in_=acc, func=ACT.Identity, bias=b1_sb[:, t : t + 1], scale=1.0)

        def scatter(t, lo, hi, h, weights):
            nc.vector.tensor_tensor(page[t][:].indirect(idx2[:, lo // 16 : hi // 16]), h[:, lo:hi], weights, ALU.mult)

        def short_unit(n, lo, hi, h):
            w = hi - lo
            val = work.tile([P, w], F32, name="short_val", bufs=3)
            product(0, lo, hi, banks[4 + n][:, :w], val[:])
            whole = work.tile([P, w], I32, name="whole")
            nc.vector.tensor_scalar(whole[:], val[:], 1.0 / TURN, None, ALU.mult)
            red = work.tile([P, w], F32, name="short_red", bufs=3)
            nc.vector.scalar_tensor_tensor(out=red[:], in0=whole[:], scalar=-TURN, in1=val[:], op0=ALU.mult, op1=ALU.add)
            mag = work.tile([P, w], F32, name="mag")
            nc.scalar.activation(out=mag[:], in_=red[:], func=ACT.Abs)
            cosv = work.tile([P, w], F32, name="short_cos", bufs=3)
            nc.scalar.activation(out=cosv[:], in_=mag[:], func=ACT.Sin, bias=math.pi / 2, scale=-1.0)
            nc.vector.scalar_tensor_tensor(
                out=h[:, lo:hi], in0=cosv[:], scalar=gain_sb[:, 0:1], in1=val[:], op0=ALU.mult, op1=ALU.mult
            )

        def long_unit(n, t, lo, hi, h):
            w = hi - lo
            val = vals[n % RING][:, :w]
            red = banks[2 + n % 2]
            cosv = banks[4 + n % 4]
            product(t, lo, hi, banks[n % 2][:, :w], val)
            turns = work.tile([P, w], U32, name="turns")
            nc.scalar.activation(out=turns[:], in_=val, func=ACT.Copy, bias=TURN_SHIFT, scale=1.0 / TURN)
            back = work.tile([P, w], F32, name="back")
            nc.scalar.activation(out=back[:], in_=turns[:], func=ACT.Copy, bias=TURN * TURN_SHIFT, scale=-TURN)
            for c in range(0, w, P):
                nc.tensor.matmul(red[:, c : c + P], val[:, c : c + P], ident[:], start=True, stop=False, is_transpose=True)
                nc.tensor.matmul(red[:, c : c + P], back[:, c : c + P], ident[:], start=False, stop=True, is_transpose=True)
            mag = work.tile([P, w], F32, name="mag")
            nc.scalar.activation(out=mag[:], in_=red[:, :w], func=ACT.Abs)
            cos_t = work.tile([P, w], F32, name="cos_t")
            nc.scalar.activation(out=cos_t[:], in_=mag[:], func=ACT.Sin, bias=math.pi / 2, scale=-1.0)
            for c in range(0, w, P):
                nc.tensor.transpose(cosv[:, c : c + P], cos_t[:, c : c + P], ident[:])
            nc.vector.scalar_tensor_tensor(
                out=h[:, lo:hi], in0=cosv[:, :w], scalar=gain_sb[:, t : t + 1], in1=val, op0=ALU.mult, op1=ALU.mult
            )

        h = work.tile([P, S], F32, name="h", tag="wide")
        for n, (lo, hi) in enumerate(J_PIECES):
            short_unit(n, lo, hi, h)
            scatter(0, lo, hi, h, wgs_first[:, lo:hi])
        for t in range(1, PACK):
            h = work.tile([P, S], F32, name="h", tag="wide")
            for lo in range(0, S, BANK):
                long_unit(2 * (t - 1) + lo // BANK, t, lo, lo + BANK, h)
                if t == 1:
                    scatter(t, lo, lo + BANK, h, wgs_rest[:, t - 1, lo : lo + BANK])
            if t > 1:
                scatter(t, 0, S, h, wgs_rest[:, t - 1, :])

        count = []
        w5_bf = head.tile([P, PACK * N], BF16, name="w5_bf", align_bytes=64, offset=0)
        w5_codes = keep.tile([P, N], U32, name="w5_codes", align_bytes=64)
        w5_plane = keep.tile([P, N], U8, name="w5_plane", align_bytes=64)
        nc.scalar.copy(
            out=w5_bf[:].rearrange("p (c e i) -> p c i e", e=4, i=PACK),
            in_=w5_raw[:].rearrange("p i (c e) -> p c i e", e=4),
        )
        nc.vector.quantize_mx(out=w5_codes[:].bitcast(FP8X4), scales=w5_plane[:], in_=w5_bf[:])

        out_rows = out.rearrange("(b p) m -> p b m", p=P)
        for lo, hi in M_PIECES:
            w = hi - lo
            x = work.tile([P, PACK, w], F32, name="x", tag="wide")
            for t in range(PACK):
                nc.vector.tensor_tensor(
                    x[:, t, :], page[t][:].indirect(idx3[:, lo // 16 : hi // 16]), wgt_sb[:, lo:hi], ALU.mult
                )
            x_bf = work.tile([P, PACK * w], BF16, name="x_bf", align_bytes=64)
            nc.scalar.copy(
                out=x_bf[:].rearrange("p (c e i) -> p c i e", e=4, i=PACK),
                in_=x[:].rearrange("p i (c e) -> p c i e", e=4),
            )
            x_codes = work.tile([P, w], U32, name="x_codes", align_bytes=64)
            x_plane = work.tile([P, w], U8, name="x_plane", align_bytes=64)
            nc.vector.quantize_mx(out=x_codes[:].bitcast(FP8X4), scales=x_plane[:], in_=x_bf[:])
            per_bank = BANK // w
            for b0 in range(0, N // P, per_bank):
                y1 = banks[2 * (len(count) % 4)]
                y2 = banks[2 * (len(count) % 4) + 1]
                count.append(b0)
                for s in range(per_bank):
                    b = b0 + s
                    nc.tensor.matmul_mx(
                        out=y1[:, s * w : (s + 1) * w],
                        lhsT=w4_codes[:, 2 * P * b : 2 * P * (b + 1)].bitcast(FP4X4),
                        lhsT_scale=w4_plane[:, P * b : P * (b + 1)],
                        rhs=x_codes[:].bitcast(FP8X4),
                        rhs_scale=x_plane[:],
                        start=True,
                        stop=True,
                    )
                for s in range(per_bank):
                    b = b0 + s
                    nc.tensor.matmul_mx(
                        out=y2[:, s * w : (s + 1) * w],
                        lhsT=w5_codes[:, P * b : P * (b + 1)].bitcast(FP8X4),
                        lhsT_scale=w5_plane[:, P * b : P * (b + 1)],
                        rhs=x_codes[:].bitcast(FP8X4),
                        rhs_scale=x_plane[:],
                        start=True,
                        stop=True,
                    )
                y1_sb = work.tile([P, BANK], F32, name="y1_sb")
                nc.scalar.copy(out=y1_sb[:], in_=y1[:])
                res = work.tile([P, BANK], F32, name="res", bufs=4)
                nc.vector.tensor_tensor(res[:], y2[:], y1_sb[:], ALU.max)
                nc.sync.dma_start(
                    out=out_rows[:, b0 : b0 + per_bank, lo:hi], in_=res[:].rearrange("p (s m) -> p s m", s=per_bank)
                )
